import numpy as np, ml_dtypes
CORES = [118,246,374,502,126,254,382,510]
N = 8
TK = 256
def setup_inputs(rng):
    return {"x": rng.standard_normal((N, 128, TK), dtype=np.float32).astype(ml_dtypes.bfloat16), "w1": rng.standard_normal((N, 128, 128), dtype=np.float32).astype(ml_dtypes.bfloat16), "w2": rng.standard_normal((N, 128, 128), dtype=np.float32).astype(ml_dtypes.bfloat16)}
def reference(x, w1, w2):
    tot = np.zeros((128, TK))
    for r in range(N):
        h = np.maximum(w1[r].astype(np.float64).T @ x[r].astype(np.float64), 0.0)
        tot += w2[r].astype(np.float64).T @ h
    s = tot.astype(ml_dtypes.bfloat16 if x.dtype != np.float64 else np.float64)
    return {"y": np.broadcast_to(s, (N,) + s.shape)}

@@ -1,0 +1,118 @@
+from concourse.bass import DstId, RemoteDMATransfer
+from concourse.mybir import AluOpType
+
+PLAN = (("cross", "switch", "mate"), ("cable",))
+NST = len(PLAN)
+HALVES = ((0, "a"), (128, "b"))
+
+SCRATCH = {
+    "xs": ("sbuf", [128, 256], "bfloat16"),
+    "w1s": ("sbuf", [128, 128], "bfloat16"),
+    "w2s": ("sbuf", [128, 128], "bfloat16"),
+    "zero": ("sbuf", [128, 128], "bfloat16"),
+    "hs": ("sbuf", [128, 256], "bfloat16"),
+    "out": ("sbuf", [128, 256], "bfloat16"),
+    "ps1a": ("psum", [128, 512], "float32"),
+    "ps1b": ("psum", [128, 512], "float32"),
+    "ps2a": ("psum", [128, 512], "float32"),
+    "ps2b": ("psum", [128, 512], "float32"),
+}
+SEMAPHORES = ["ld_w1", "ld_x", "ld_w2", "zf", "m1a", "m1b", "ha", "hb", "m2a", "m2b", "va", "vb", "sent", "st"]
+for _k, _rels in enumerate(PLAN):
+    SCRATCH["snd%d" % _k] = ("sbuf", [128, 256], "bfloat16")
+    SEMAPHORES.append("arr%d" % _k)
+    for _rel in _rels:
+        SCRATCH["r%d_%s" % (_k, _rel)] = ("sbuf", [128, 256], "bfloat16")
+for _k in range(NST + 1):
+    SEMAPHORES.append("rdy%da" % _k)
+    SEMAPHORES.append("rdy%db" % _k)
+
+
+def _partner(core, rel):
+    h, ch, k = core // 128, (core % 128) // 8, core % 8
+    if rel == "mate":
+        ch ^= 1
+    elif rel == "switch":
+        h ^= 1
+    elif rel == "cross":
+        h ^= 1
+        ch ^= 1
+    elif rel == "cable":
+        h = 3 - h
+    return h * 128 + ch * 8 + k
+
+
+def rank_program(g, core, T, topo):
+    if T.rank_of(core) is None:
+        return
+    S = T.sem
+    ten, vec = g.tensor, g.vector
+    ps1 = {"a": T.ps1a, "b": T.ps1b}
+    ps2 = {"a": T.ps2a, "b": T.ps2b}
+
+    g.sync.dma_start(T.w1s[:], T.w1[:]).then_inc(S.ld_w1, 16)
+    g.scalar.dma_start(T.xs[:], T.x[:]).then_inc(S.ld_x, 16)
+    g.sync.dma_start(T.w2s[:], T.w2[:]).then_inc(S.ld_w2, 16)
+    vec.memset(T.zero[:], 0.0).then_inc(S.zf, 1)
+    vec.wait_ge(S.zf, 1)
+
+    ten.wait_ge(S.ld_w1, 16)
+    ten.wait_ge(S.ld_x, 16)
+    for c0, n in HALVES:
+        ten.matmul(ps1[n][:, 0:128], T.w1s[:], T.xs[:, c0:c0 + 128], start=True, stop=True).then_inc(S["m1" + n], 1)
+    for c0, n in HALVES:
+        vec.wait_ge(S["m1" + n], 1)
+        vec.tensor_tensor(T.hs[:, c0:c0 + 128], ps1[n][:, 0:128], T.zero[:], AluOpType.max).then_inc(S["h" + n], 1)
+    ten.wait_ge(S.ld_w2, 16)
+    for c0, n in HALVES:
+        ten.wait_ge(S["h" + n], 1)
+        ten.matmul(ps2[n][:, 0:128], T.w2s[:], T.hs[:, c0:c0 + 128], start=True, stop=True).then_inc(S["m2" + n], 1)
+    for c0, n in HALVES:
+        vec.wait_ge(S["m2" + n], 1)
+        vec.tensor_copy(T.snd0[:, c0:c0 + 128], ps2[n][:, 0:128]).then_inc(S["rdy0" + n], 1)
+
+    cnt = {"a": 0, "b": 0}
+    sent = 0
+    for c0, n in HALVES:
+        vec.wait_ge(S["rdy0" + n], 1)
+    for k, rels in enumerate(PLAN):
+        for c0, n in HALVES:
+            g.wait_ge(S["rdy%d%s" % (k, n)], 1)
+        ids, dsts = [], []
+        for rel in rels:
+            rid, pid = topo.addr(_partner(core, rel), core)
+            ids.append(DstId(rid=rid, pnc=pid))
+            dsts.append(T["r%d_%s" % (k, rel)][:])
+        g.remote_dma_fused(
+            [RemoteDMATransfer(dst_ids=ids, dma_engine_mask=0xFF, remote_sem=S["arr%d" % k],
+                               srcs=[T["snd%d" % k][:]], dsts=dsts, alu_op=0)],
+            local_sem=S.sent)
+        sent += 8
+
+        vec.wait_ge(S["arr%d" % k], 8 * len(rels))
+        nxt = T.out if k == NST - 1 else T["snd%d" % (k + 1)]
+        for j, rel in enumerate(rels):
+            r = T["r%d_%s" % (k, rel)]
+            for c0, n in HALVES:
+                acc = ps2[n][:, 0:128]
+                if cnt[n]:
+                    vec.wait_ge(S["v" + n], cnt[n])
+                if j < len(rels) - 1:
+                    vec.tensor_tensor(acc, acc, r[:, c0:c0 + 128], AluOpType.add).then_inc(S["v" + n], 1)
+                    cnt[n] += 1
+                else:
+                    vec.tensor_tensor(nxt[:, c0:c0 + 128], acc, r[:, c0:c0 + 128], AluOpType.add).then_inc(
+                        S["rdy%d%s" % (k + 1, n)], 1)
+        if k < NST - 1:
+            r = T["r%d_%s" % (k, rels[-1])]
+            for c0, n in HALVES:
+                acc = ps2[n][:, 0:128]
+                vec.wait_ge(S["rdy%d%s" % (k + 1, n)], 1)
+                vec.tensor_tensor(acc, acc, r[:, c0:c0 + 128], AluOpType.add).then_inc(S["v" + n], 1)
+                cnt[n] += 1
+
+    for c0, n in HALVES:
+        g.sync.wait_ge(S["rdy%d%s" % (NST, n)], 1)
+    g.sync.dma_start(T.y[:], T.out[:]).then_inc(S.st, 16)
+    g.sync.wait_ge(S.st, 16)
+    g.wait_ge(S.sent, sent)

@@ -1,8 +1,7 @@
 from concourse.bass import DstId, RemoteDMATransfer
 from concourse.mybir import AluOpType
 
-PLAN = (("cross", "switch", "mate"), ("cable",))
-NST = len(PLAN)
+RELS0 = ("cross", "switch", "mate")
 HALVES = ((0, "a"), (128, "b"))
 
 SCRATCH = {
@@ -11,21 +10,20 @@ SCRATCH = {
     "w2s": ("sbuf", [128, 128], "bfloat16"),
     "zero": ("sbuf", [128, 128], "bfloat16"),
     "hs": ("sbuf", [128, 256], "bfloat16"),
+    "ps": ("sbuf", [128, 256], "bfloat16"),
+    "r_cross": ("sbuf", [128, 256], "bfloat16"),
+    "r_switch": ("sbuf", [128, 256], "bfloat16"),
+    "r_mate": ("sbuf", [128, 256], "bfloat16"),
+    "r_cable": ("sbuf", [128, 256], "bfloat16"),
     "out": ("sbuf", [128, 256], "bfloat16"),
     "ps1a": ("psum", [128, 512], "float32"),
     "ps1b": ("psum", [128, 512], "float32"),
     "ps2a": ("psum", [128, 512], "float32"),
     "ps2b": ("psum", [128, 512], "float32"),
+    "ps3": ("psum", [128, 512], "float32"),
 }
-SEMAPHORES = ["ld_w1", "ld_x", "ld_w2", "zf", "m1a", "m1b", "ha", "hb", "m2a", "m2b", "va", "vb", "sent", "st"]
-for _k, _rels in enumerate(PLAN):
-    SCRATCH["snd%d" % _k] = ("sbuf", [128, 256], "bfloat16")
-    SEMAPHORES.append("arr%d" % _k)
-    for _rel in _rels:
-        SCRATCH["r%d_%s" % (_k, _rel)] = ("sbuf", [128, 256], "bfloat16")
-for _k in range(NST + 1):
-    SEMAPHORES.append("rdy%da" % _k)
-    SEMAPHORES.append("rdy%db" % _k)
+SEMAPHORES = ["ld_w1", "ld_x", "ld_w2", "zf", "m1a", "m1b", "ha", "hb", "m2a", "m2b", "pa", "pb", "va", "vb",
+              "arr0", "arr1", "fin", "sent", "st"]
 
 
 def _partner(core, rel):
@@ -50,6 +48,10 @@ def rank_program(g, core, T, topo):
     ps1 = {"a": T.ps1a, "b": T.ps1b}
     ps2 = {"a": T.ps2a, "b": T.ps2b}
 
+    def dst_id(rel):
+        rid, pid = topo.addr(_partner(core, rel), core)
+        return DstId(rid=rid, pnc=pid)
+
     g.sync.dma_start(T.w1s[:], T.w1[:]).then_inc(S.ld_w1, 16)
     g.scalar.dma_start(T.xs[:], T.x[:]).then_inc(S.ld_x, 16)
     g.sync.dma_start(T.w2s[:], T.w2[:]).then_inc(S.ld_w2, 16)
@@ -69,50 +71,38 @@ def rank_program(g, core, T, topo):
         ten.matmul(ps2[n][:, 0:128], T.w2s[:], T.hs[:, c0:c0 + 128], start=True, stop=True).then_inc(S["m2" + n], 1)
     for c0, n in HALVES:
         vec.wait_ge(S["m2" + n], 1)
-        vec.tensor_copy(T.snd0[:, c0:c0 + 128], ps2[n][:, 0:128]).then_inc(S["rdy0" + n], 1)
+        vec.tensor_copy(T.ps[:, c0:c0 + 128], ps2[n][:, 0:128]).then_inc(S["p" + n], 1)
 
-    cnt = {"a": 0, "b": 0}
-    sent = 0
     for c0, n in HALVES:
-        vec.wait_ge(S["rdy0" + n], 1)
-    for k, rels in enumerate(PLAN):
+        g.wait_ge(S["p" + n], 1)
+    g.remote_dma_fused(
+        [RemoteDMATransfer(dst_ids=[dst_id(rel) for rel in RELS0], dma_engine_mask=0xFF, remote_sem=S.arr0,
+                           srcs=[T.ps[:]], dsts=[T["r_" + rel][:] for rel in RELS0], alu_op=0)],
+        local_sem=S.sent)
+
+    g.wait_ge(S.arr0, 8 * len(RELS0))
+    g.remote_dma_fused(
+        [RemoteDMATransfer(dst_ids=[dst_id("cable")], dma_engine_mask=0xFF, remote_sem=S.arr1,
+                           srcs=[T.ps[:]] + [T["r_" + rel][:] for rel in RELS0], dsts=[T.r_cable[:]], alu_op=1)],
+        local_sem=S.sent)
+
+    for c0, n in HALVES:
+        vec.wait_ge(S["p" + n], 1)
+    vec.wait_ge(S.arr0, 8 * len(RELS0))
+    for j, rel in enumerate(RELS0):
+        r = T["r_" + rel]
         for c0, n in HALVES:
-            g.wait_ge(S["rdy%d%s" % (k, n)], 1)
-        ids, dsts = [], []
-        for rel in rels:
-            rid, pid = topo.addr(_partner(core, rel), core)
-            ids.append(DstId(rid=rid, pnc=pid))
-            dsts.append(T["r%d_%s" % (k, rel)][:])
-        g.remote_dma_fused(
-            [RemoteDMATransfer(dst_ids=ids, dma_engine_mask=0xFF, remote_sem=S["arr%d" % k],
-                               srcs=[T["snd%d" % k][:]], dsts=dsts, alu_op=0)],
-            local_sem=S.sent)
-        sent += 8
-
-        vec.wait_ge(S["arr%d" % k], 8 * len(rels))
-        nxt = T.out if k == NST - 1 else T["snd%d" % (k + 1)]
-        for j, rel in enumerate(rels):
-            r = T["r%d_%s" % (k, rel)]
-            for c0, n in HALVES:
-                acc = ps2[n][:, 0:128]
-                if cnt[n]:
-                    vec.wait_ge(S["v" + n], cnt[n])
-                if j < len(rels) - 1:
-                    vec.tensor_tensor(acc, acc, r[:, c0:c0 + 128], AluOpType.add).then_inc(S["v" + n], 1)
-                    cnt[n] += 1
-                else:
-                    vec.tensor_tensor(nxt[:, c0:c0 + 128], acc, r[:, c0:c0 + 128], AluOpType.add).then_inc(
-                        S["rdy%d%s" % (k + 1, n)], 1)
-        if k < NST - 1:
-            r = T["r%d_%s" % (k, rels[-1])]
-            for c0, n in HALVES:
-                acc = ps2[n][:, 0:128]
-                vec.wait_ge(S["rdy%d%s" % (k + 1, n)], 1)
-                vec.tensor_tensor(acc, acc, r[:, c0:c0 + 128], AluOpType.add).then_inc(S["v" + n], 1)
-                cnt[n] += 1
-
+            acc = ps2[n][:, 0:128]
+            if j:
+                vec.wait_ge(S["v" + n], j)
+            o = acc if j < len(RELS0) - 1 else T.ps3[:, c0:c0 + 128]
+            vec.tensor_tensor(o, acc, r[:, c0:c0 + 128], AluOpType.add).then_inc(S["v" + n], 1)
     for c0, n in HALVES:
-        g.sync.wait_ge(S["rdy%d%s" % (NST, n)], 1)
+        vec.wait_ge(S["v" + n], len(RELS0))
+
+    vec.wait_ge(S.arr1, 8)
+    vec.tensor_tensor(T.out[:], T.ps3[:, 0:256], T.r_cable[:], AluOpType.add).then_inc(S.fin, 1)
+    g.sync.wait_ge(S.fin, 1)
     g.sync.dma_start(T.y[:], T.out[:]).then_inc(S.st, 16)
     g.sync.wait_ge(S.st, 16)
-    g.wait_ge(S.sent, sent)
+    g.wait_ge(S.sent, 16)

from concourse.bass import DstId, RemoteDMATransfer
from concourse.mybir import AluOpType

RELS0 = ("cross", "switch", "mate")
HALVES = ((0, "a"), (128, "b"))

SCRATCH = {
    "xs": ("sbuf", [128, 256], "bfloat16"),
    "w1s": ("sbuf", [128, 128], "bfloat16"),
    "w2s": ("sbuf", [128, 128], "bfloat16"),
    "zero": ("sbuf", [128, 128], "bfloat16"),
    "hs": ("sbuf", [128, 256], "bfloat16"),
    "ps": ("sbuf", [128, 256], "bfloat16"),
    "r_cross": ("sbuf", [128, 256], "bfloat16"),
    "r_switch": ("sbuf", [128, 256], "bfloat16"),
    "r_mate": ("sbuf", [128, 256], "bfloat16"),
    "r_cable": ("sbuf", [128, 256], "bfloat16"),
    "out": ("sbuf", [128, 256], "bfloat16"),
    "ps1a": ("psum", [128, 512], "float32"),
    "ps1b": ("psum", [128, 512], "float32"),
    "ps2a": ("psum", [128, 512], "float32"),
    "ps2b": ("psum", [128, 512], "float32"),
    "ps3": ("psum", [128, 512], "float32"),
}
SEMAPHORES = ["ld_w1", "ld_x", "ld_w2", "zf", "m1a", "m1b", "ha", "hb", "m2a", "m2b", "pa", "pb", "va", "vb",
              "arr0", "arr1", "fin", "sent", "st"]


def _partner(core, rel):
    h, ch, k = core // 128, (core % 128) // 8, core % 8
    if rel == "mate":
        ch ^= 1
    elif rel == "switch":
        h ^= 1
    elif rel == "cross":
        h ^= 1
        ch ^= 1
    elif rel == "cable":
        h = 3 - h
    return h * 128 + ch * 8 + k


def rank_program(g, core, T, topo):
    if T.rank_of(core) is None:
        return
    S = T.sem
    ten, vec = g.tensor, g.vector
    ps1 = {"a": T.ps1a, "b": T.ps1b}
    ps2 = {"a": T.ps2a, "b": T.ps2b}

    def dst_id(rel):
        rid, pid = topo.addr(_partner(core, rel), core)
        return DstId(rid=rid, pnc=pid)

    g.sync.dma_start(T.w1s[:], T.w1[:]).then_inc(S.ld_w1, 16)
    g.scalar.dma_start(T.xs[:], T.x[:]).then_inc(S.ld_x, 16)
    g.sync.dma_start(T.w2s[:], T.w2[:]).then_inc(S.ld_w2, 16)
    vec.memset(T.zero[:], 0.0).then_inc(S.zf, 1)
    vec.wait_ge(S.zf, 1)

    ten.wait_ge(S.ld_w1, 16)
    ten.wait_ge(S.ld_x, 16)
    for c0, n in HALVES:
        ten.matmul(ps1[n][:, 0:128], T.w1s[:], T.xs[:, c0:c0 + 128], start=True, stop=True).then_inc(S["m1" + n], 1)
    for c0, n in HALVES:
        vec.wait_ge(S["m1" + n], 1)
        vec.tensor_tensor(T.hs[:, c0:c0 + 128], ps1[n][:, 0:128], T.zero[:], AluOpType.max).then_inc(S["h" + n], 1)
    ten.wait_ge(S.ld_w2, 16)
    for c0, n in HALVES:
        ten.wait_ge(S["h" + n], 1)
        ten.matmul(ps2[n][:, 0:128], T.w2s[:], T.hs[:, c0:c0 + 128], start=True, stop=True).then_inc(S["m2" + n], 1)
    for c0, n in HALVES:
        vec.wait_ge(S["m2" + n], 1)
        vec.tensor_copy(T.ps[:, c0:c0 + 128], ps2[n][:, 0:128]).then_inc(S["p" + n], 1)

    for c0, n in HALVES:
        g.wait_ge(S["p" + n], 1)
    g.remote_dma_fused(
        [RemoteDMATransfer(dst_ids=[dst_id(rel) for rel in RELS0], dma_engine_mask=0xFF, remote_sem=S.arr0,
                           srcs=[T.ps[:]], dsts=[T["r_" + rel][:] for rel in RELS0], alu_op=0)],
        local_sem=S.sent)

    g.wait_ge(S.arr0, 8 * len(RELS0))
    g.remote_dma_fused(
        [RemoteDMATransfer(dst_ids=[dst_id("cable")], dma_engine_mask=0xFF, remote_sem=S.arr1,
                           srcs=[T.ps[:]] + [T["r_" + rel][:] for rel in RELS0], dsts=[T.r_cable[:]], alu_op=1)],
        local_sem=S.sent)

    for c0, n in HALVES:
        vec.wait_ge(S["p" + n], 1)
    vec.wait_ge(S.arr0, 8 * len(RELS0))
    for j, rel in enumerate(RELS0):
        r = T["r_" + rel]
        for c0, n in HALVES:
            acc = ps2[n][:, 0:128]
            if j:
                vec.wait_ge(S["v" + n], j)
            o = acc if j < len(RELS0) - 1 else T.ps3[:, c0:c0 + 128]
            vec.tensor_tensor(o, acc, r[:, c0:c0 + 128], AluOpType.add).then_inc(S["v" + n], 1)
    for c0, n in HALVES:
        vec.wait_ge(S["v" + n], len(RELS0))

    vec.wait_ge(S.arr1, 8)
    vec.tensor_tensor(T.out[:], T.ps3[:, 0:256], T.r_cable[:], AluOpType.add).then_inc(S.fin, 1)
    g.sync.wait_ge(S.fin, 1)
    g.sync.dma_start(T.y[:], T.out[:]).then_inc(S.st, 16)
    g.sync.wait_ge(S.st, 16)
    g.wait_ge(S.sent, 16)
